import numpy as np
import ml_dtypes


def mxq(x, axis, fmt="e4m3"):
    dtype, down = {"e4m3": (ml_dtypes.float8_e4m3fn, 7), "e5m2": (ml_dtypes.float8_e5m2, 14)}[fmt]
    v = np.moveaxis(np.asarray(x, np.float32).astype(ml_dtypes.bfloat16).astype(np.float64), axis, -1)
    blocks = v.reshape(v.shape[:-1] + (-1, 32))
    amax = np.abs(blocks).max(-1, keepdims=True)
    byte = np.maximum(np.where(amax > 0, np.frexp(amax)[1] - 1 + 127, 0) - down, 1)
    scale = np.exp2(byte - 127.0)
    codes = (blocks / scale).astype(np.float32).astype(dtype).astype(np.float64)
    return np.moveaxis((codes * scale).reshape(v.shape), -1, axis)


WIDE = False


def mx_kscale(k):
    if not WIDE:
        return np.ones(k)
    levels = np.array([10, -10, 5, -5, 0])
    if k % 512:
        return np.exp2(np.random.permutation(np.resize(levels, k // 32))).repeat(32)
    a = np.empty((k // 512, 16))
    for p in range(k // 512):
        a[p, :8] = np.random.permutation(np.resize(levels, 8))
        for g in range(8):
            far = levels[np.abs(levels - a[p, g]) >= 10]
            a[p, g + 8] = far[np.random.randint(len(far))]
    return np.exp2(a.ravel()).repeat(32)


def f64(x):
    return np.asarray(x).astype(np.float64)


def striped(idx):
    return np.tile(idx.reshape(-1, 16).T, (8, 1)).astype(np.uint16)


def unstriped(offs):
    return offs[:16].T.reshape(-1).astype(np.int64)


def pack_weight(w):
    k, n = w.shape
    w = f64(np.asarray(w, np.float32).astype(ml_dtypes.bfloat16)).reshape(k // 32, 32, n)
    amax = np.abs(w).max(1)
    byte = np.clip(np.where(amax > 0, np.frexp(amax)[1] - 1 + 127 - 7, 1), 1, 254)
    scaled = (w * np.exp2(127.0 - byte)[:, None, :]).reshape(k, n).astype(np.float32)
    words = np.ascontiguousarray(scaled.reshape(k // 512, 128, 4, n).transpose(0, 1, 3, 2)).astype(ml_dtypes.float8_e4m3fn).view(np.uint8)
    return words, np.ascontiguousarray(byte.astype(np.uint8).reshape(k // 512, 16, n))


def unpack_weight(words, scales):
    g, p, n, _ = words.shape
    vals = np.ascontiguousarray(words).view(ml_dtypes.float8_e4m3fn).astype(np.float64) * np.repeat(np.exp2(scales.astype(np.float64) - 127.0), 8, axis=1)[..., None]
    return vals.transpose(0, 1, 3, 2).reshape(g * 512, n)


def gelu(v):
    return 0.5 * v * (1.0 + np.tanh(np.sqrt(2.0 / np.pi) * (v + 0.044715 * v**3)))


K, T, E, C, N = 1536, 512, 8, 128, 256


def by_expert(wq, xq):
    return np.concatenate([wq[e].T @ xq[:, e * C:(e + 1) * C] for e in range(E)], axis=1)


def setup_inputs():
    n = np.random.standard_normal
    s = mx_kscale(K)[:, None]
    first = np.random.permutation(np.repeat(np.arange(E), T // E))
    second = (first + 1 + np.random.permutation(np.repeat(np.arange(E - 1), -(-T // (E - 1)))[:T])) % E
    while np.bincount(second, minlength=E).max() != T // E:
        load = np.bincount(second, minlength=E); hi, lo = int(load.argmax()), int(load.argmin())
        t = np.flatnonzero((second == hi) & (first != lo))[0]; second[t] = lo
    slot_token = np.empty(E * C, np.int64); pos = np.empty((2, T), np.int64); fill = np.zeros(E, np.int64)
    place = np.stack([np.random.permutation(C) for _ in range(E)])
    for r, deal in enumerate((first, second)):
        for t in np.random.permutation(T):
            e = deal[t]; j = e * C + place[e, fill[e]]; fill[e] += 1; slot_token[j] = t; pos[r, t] = j
    g = np.random.uniform(0.2, 0.8, T)
    packed = [pack_weight(m) for m in n((E, K, N)) / np.sqrt(K) / s[None]]
    return {
        "xT": (n((K, T)) * s).astype(np.float32),
        "w_words": np.stack([m[0] for m in packed]),
        "w_scales": np.stack([m[1] for m in packed]),
        "b": (0.3 * n((N, E))).astype(np.float32),
        "gate": np.stack([np.tile(g, (N, 1)), np.tile(1.0 - g, (N, 1))]).astype(np.float32),
        "offs": striped(slot_token),
        "pos1": striped(pos[0]),
        "pos2": striped(pos[1]),
    }


def reference(xT, w_words, w_scales, b, gate, offs, pos1, pos2):
    idx = unstriped(offs)
    xq = mxq(f64(xT)[:, idx], 0, "e4m3")
    w = np.stack([unpack_weight(w_words[e], w_scales[e]) for e in range(E)])
    y = by_expert(w, xq)
    y = gelu(y + np.repeat(f64(b), C, axis=1))
    return f64(gate[0]) * y[:, unstriped(pos1)] + f64(gate[1]) * y[:, unstriped(pos2)]

@@ -1,0 +1,134 @@
+from contextlib import ExitStack
+
+import concourse.mybir as mybir
+
+K, T, E, C, N = 1536, 512, 8, 128, 256
+P = 128
+PASSES = K // 512
+SLOTS = E * C
+FLOPS = 2 * K * N * SLOTS
+
+F32 = mybir.dt.float32
+BF16 = mybir.dt.bfloat16
+I32 = mybir.dt.int32
+U32 = mybir.dt.uint32
+U16 = mybir.dt.uint16
+U8 = mybir.dt.uint8
+FP8X4 = mybir.dt.float8_e4m3fn_x4
+GELU = mybir.ActivationFunctionType.Gelu_apprx_tanh
+MULT = mybir.AluOpType.mult
+
+
+def tile_routed_moe_kernel(tc, xT, w_words, w_scales, b, gate, offs, pos1, pos2, out):
+    nc = tc.nc
+    with ExitStack() as ctx:
+        keep = ctx.enter_context(tc.tile_pool(name="keep", bufs=1))
+        psum = ctx.enter_context(tc.psum_pool(name="psum", bufs=8))
+
+        x_planes = xT.rearrange("(g p t) n -> g p t n", p=P, t=4)
+        w_rows = w_words.rearrange("e a p n r -> p (e a) (n r)").bitcast(I32)
+        s_rows = w_scales.bitcast(I32)
+
+        offs_sb = keep.tile([P, SLOTS // 16], U16, name="offs_sb")
+        pos_sb = [keep.tile([P, T // 16], U16, name=f"pos{r}_sb") for r in range(2)]
+        b_sb = keep.tile([P, 2, E], F32, name="b_sb")
+        warm = keep.tile([P, 1], F32, name="warm")
+        raw = {}
+        for g in range(PASSES):
+            for h in range(2):
+                raw[g, h] = keep.tile([P, 4, T // 2], F32, name=f"raw{g}_{h}")
+        words = [keep.tile([P, 2048], I32, name=f"words{g}", align_bytes=64) for g in range(PASSES)]
+        scales = keep.tile([P, T], U8, name="scales", align_bytes=64)
+        slot_words = [keep.tile([P, SLOTS], U32, name=f"slot_words{g}", align_bytes=64) for g in range(PASSES)]
+        slot_scales = keep.tile([P, SLOTS], U8, name="slot_scales", align_bytes=64)
+        w_sb = [keep.tile([P, 6, N], I32, name=f"w_sb{i}", align_bytes=64) for i in range(E // 2)]
+        ws_sb = keep.tile([P, E, N // 4], I32, name="ws_sb", align_bytes=64)
+        gate_sb = [[keep.tile([P, T], F32, name=f"gate{r}_{m}") for m in range(2)] for r in range(2)]
+        y = [keep.tile([P, SLOTS], F32, name=f"y{m}") for m in range(2)]
+
+        nc.vector.memset(warm[:], 0.0)
+        nc.scalar.activation(warm[:], warm[:], GELU)
+        nc.vector.memset(ws_sb[:], 0)
+        nc.gpsimd.memset(scales[:], 0)
+        for g in range(PASSES):
+            nc.vector.memset(words[g][:, T:], 0)
+
+        nc.gpsimd.dma_start(b_sb[:], b.rearrange("(m p) e -> p m e", p=P))
+
+        def load_x(g):
+            for h in range(2):
+                nc.sync.dma_start(raw[g, h][:], x_planes[g, :, :, h * (T // 2):(h + 1) * (T // 2)])
+
+        def load_scales(n0, n1):
+            for i in range(n0, n1):
+                a, q = divmod(i, 4)
+                nc.sync.dma_start(ws_sb[32 * q + 4 * a:32 * q + 4 * a + 4], s_rows[:, a, 4 * q:4 * q + 4, :].rearrange("e r n -> r e n"))
+
+        load_x(0)
+        nc.sync.dma_start(offs_sb[:], offs)
+        load_x(1)
+        load_scales(0, 4)
+        load_x(2)
+        load_scales(4, 12)
+        for i in range(E // 2):
+            nc.sync.dma_start(w_sb[i][:], w_rows[:, 6 * i:6 * i + 6, :])
+        nc.sync.dma_start(pos_sb[0][:], pos1)
+        nc.sync.dma_start(pos_sb[1][:], pos2)
+        for m in range(2):
+            for r in range(2):
+                nc.sync.dma_start(gate_sb[r][m][:], gate[r, m * P:(m + 1) * P, :])
+
+        def quantise(g):
+            for h in range(2):
+                grouped = keep.tile([P, T // 2, 4], BF16, name=f"grouped{g}_{h}", align_bytes=64)
+                dst = grouped[:].rearrange("p (c i) t -> p c t i", i=4)
+                src = raw[g, h][:].rearrange("p t (c i) -> p c t i", i=4)
+                if g == 0 and h == 0:
+                    nc.vector.tensor_copy(dst, src)
+                else:
+                    nc.scalar.copy(dst, src)
+                cols = slice(h * (T // 2), (h + 1) * (T // 2))
+                nc.vector.quantize_mx(out=words[g][:, cols].bitcast(FP8X4), scales=scales[4 * g:P, cols], in_=grouped[:].rearrange("p n t -> p (n t)"))
+
+        def gather_words(g, s0, s1):
+            nc.vector.tensor_copy(slot_words[g][:, s0:s1], words[g][:].bitcast(U32).indirect(offs_sb[:, s0 // 16:s1 // 16]))
+
+        def gather_scales(s0, s1):
+            nc.vector.tensor_copy(slot_scales[:, s0:s1], scales[:].indirect(offs_sb[:, s0 // 16:s1 // 16]))
+
+        quantise(0)
+        gather_words(0, 0, SLOTS)
+        quantise(1)
+        gather_words(1, 0, SLOTS)
+        quantise(2)
+        for s in range(0, SLOTS, 256):
+            gather_scales(s, s + 256)
+            gather_words(2, s, s + 256)
+
+        ws_u8 = ws_sb[:].rearrange("p e n -> p (e n)").bitcast(U8)
+        for m in range(2):
+            for e in range(E):
+                acc = psum.tile([P, C], F32, name="acc")
+                slots = slice(e * C, (e + 1) * C)
+                for a in range(PASSES):
+                    nc.tensor.matmul_mx(
+                        out=acc[:],
+                        lhsT=w_sb[e // 2][:, 3 * (e % 2) + a, m * P:(m + 1) * P].bitcast(FP8X4),
+                        lhsT_scale=ws_u8[4 * a:P, e * N + m * P:e * N + (m + 1) * P],
+                        rhs=slot_words[a][:, slots].bitcast(FP8X4),
+                        rhs_scale=slot_scales[4 * a:P, slots],
+                        start=(a == 0),
+                        stop=(a == PASSES - 1),
+                    )
+                nc.scalar.activation(y[m][:, slots], acc[:], GELU, bias=b_sb[:, m, e:e + 1])
+
+        for m in range(2):
+            for h0, h1 in ([(0, T)] if m == 0 else [(0, 256), (256, T)]):
+                parts = []
+                for r in range(2):
+                    part = keep.tile([P, h1 - h0], F32, name=f"part{m}_{h0}_{r}")
+                    nc.vector.tensor_tensor(part[:], y[m][:].indirect(pos_sb[r][:, h0 // 16:h1 // 16]), gate_sb[r][m][:, h0:h1], MULT)
+                    parts.append(part)
+                total = keep.tile([P, h1 - h0], F32, name=f"total{m}_{h0}")
+                nc.vector.tensor_add(total[:], parts[0][:], parts[1][:])
+                nc.sync.dma_start(out[m * P:(m + 1) * P, h0:h1], total[:])

@@ -7,6 +7,7 @@ P = 128
 PASSES = K // 512
 SLOTS = E * C
 FLOPS = 2 * K * N * SLOTS
+WINDOW = 1376
 
 F32 = mybir.dt.float32
 BF16 = mybir.dt.bfloat16
@@ -27,68 +28,72 @@ def tile_routed_moe_kernel(tc, xT, w_words, w_scales, b, gate, offs, pos1, pos2,
 
         x_planes = xT.rearrange("(g p t) n -> g p t n", p=P, t=4)
         w_rows = w_words.rearrange("e a p n r -> p (e a) (n r)").bitcast(I32)
-        s_rows = w_scales.bitcast(I32)
+        s_rows = w_scales.rearrange("e a (q r) n -> r q (e a) n", r=4).bitcast(I32)
 
         offs_sb = keep.tile([P, SLOTS // 16], U16, name="offs_sb")
         pos_sb = [keep.tile([P, T // 16], U16, name=f"pos{r}_sb") for r in range(2)]
         b_sb = keep.tile([P, 2, E], F32, name="b_sb")
         warm = keep.tile([P, 1], F32, name="warm")
-        raw = {}
-        for g in range(PASSES):
-            for h in range(2):
-                raw[g, h] = keep.tile([P, 4, T // 2], F32, name=f"raw{g}_{h}")
-        words = [keep.tile([P, 2048], I32, name=f"words{g}", align_bytes=64) for g in range(PASSES)]
+        raw = [keep.tile([P, 4, T], F32, name=f"raw{g}") for g in range(PASSES)]
+        grouped = [keep.tile([P, T, 4], BF16, name=f"grouped{g}", align_bytes=64) for g in range(PASSES)]
+        words = [keep.tile([P, WINDOW], I32, name=f"words{g}", align_bytes=64) for g in range(PASSES)]
         scales = keep.tile([P, T], U8, name="scales", align_bytes=64)
         slot_words = [keep.tile([P, SLOTS], U32, name=f"slot_words{g}", align_bytes=64) for g in range(PASSES)]
         slot_scales = keep.tile([P, SLOTS], U8, name="slot_scales", align_bytes=64)
         w_sb = [keep.tile([P, 6, N], I32, name=f"w_sb{i}", align_bytes=64) for i in range(E // 2)]
-        ws_sb = keep.tile([P, E, N // 4], I32, name="ws_sb", align_bytes=64)
-        gate_sb = [[keep.tile([P, T], F32, name=f"gate{r}_{m}") for m in range(2)] for r in range(2)]
+        ws_sb = keep.tile([P, 3 * E, N // 4], I32, name="ws_sb", align_bytes=64)
+        gate_sb = [keep.tile([P, 2, T], F32, name=f"gate{m}") for m in range(2)]
         y = [keep.tile([P, SLOTS], F32, name=f"y{m}") for m in range(2)]
 
         nc.vector.memset(warm[:], 0.0)
         nc.scalar.activation(warm[:], warm[:], GELU)
+        nc.vector.memset(scales[:].bitcast(I32), 0)
         nc.vector.memset(ws_sb[:], 0)
-        nc.gpsimd.memset(scales[:], 0)
         for g in range(PASSES):
             nc.vector.memset(words[g][:, T:], 0)
 
-        nc.gpsimd.dma_start(b_sb[:], b.rearrange("(m p) e -> p m e", p=P))
 
-        def load_x(g):
-            for h in range(2):
-                nc.sync.dma_start(raw[g, h][:], x_planes[g, :, :, h * (T // 2):(h + 1) * (T // 2)])
+        def load_x(g, pieces):
+            step = T // pieces
+            for n0 in range(0, T, step):
+                nc.sync.dma_start(raw[g][:, :, n0:n0 + step], x_planes[g, :, :, n0:n0 + step])
 
-        def load_scales(n0, n1):
-            for i in range(n0, n1):
-                a, q = divmod(i, 4)
-                nc.sync.dma_start(ws_sb[32 * q + 4 * a:32 * q + 4 * a + 4], s_rows[:, a, 4 * q:4 * q + 4, :].rearrange("e r n -> r e n"))
-
-        load_x(0)
-        nc.sync.dma_start(offs_sb[:], offs)
-        load_x(1)
-        load_scales(0, 4)
-        load_x(2)
-        load_scales(4, 12)
-        for i in range(E // 2):
+        def load_w(i):
             nc.sync.dma_start(w_sb[i][:], w_rows[:, 6 * i:6 * i + 6, :])
+
+        def load_ws():
+            for r in range(4):
+                nc.sync.dma_start(ws_sb[r:P:32, :, :], s_rows[r])
+
+        def load_gate(m):
+            nc.sync.dma_start(gate_sb[m][:], gate[:, m * P:(m + 1) * P, :].rearrange("r p t -> p r t"))
+
+        load_x(0, 2)
+        nc.sync.dma_start(offs_sb[:], offs)
+        load_x(1, 1)
+        load_x(2, 1)
+        load_w(0)
+        load_ws()
+        nc.sync.dma_start(b_sb[:], b.rearrange("(m p) e -> p m e", p=P))
+        load_w(1)
+        load_w(2)
+        load_w(3)
         nc.sync.dma_start(pos_sb[0][:], pos1)
         nc.sync.dma_start(pos_sb[1][:], pos2)
-        for m in range(2):
-            for r in range(2):
-                nc.sync.dma_start(gate_sb[r][m][:], gate[r, m * P:(m + 1) * P, :])
+        load_gate(0)
+        load_gate(1)
 
-        def quantise(g):
-            for h in range(2):
-                grouped = keep.tile([P, T // 2, 4], BF16, name=f"grouped{g}_{h}", align_bytes=64)
-                dst = grouped[:].rearrange("p (c i) t -> p c t i", i=4)
-                src = raw[g, h][:].rearrange("p t (c i) -> p c t i", i=4)
-                if g == 0 and h == 0:
-                    nc.vector.tensor_copy(dst, src)
-                else:
-                    nc.scalar.copy(dst, src)
-                cols = slice(h * (T // 2), (h + 1) * (T // 2))
-                nc.vector.quantize_mx(out=words[g][:, cols].bitcast(FP8X4), scales=scales[4 * g:P, cols], in_=grouped[:].rearrange("p n t -> p (n t)"))
+        def interleave(copy, g, n0, n1):
+            copy(grouped[g][:, n0:n1, :].rearrange("p (c i) t -> p c t i", i=4), raw[g][:, :, n0:n1].rearrange("p t (c i) -> p c t i", i=4))
+
+        def quantise(g, h, on_vector):
+            n0, n1 = h * (T // 2), (h + 1) * (T // 2)
+            cut = n0 + on_vector
+            if cut > n0:
+                interleave(nc.vector.tensor_copy, g, n0, cut)
+            if cut < n1:
+                interleave(nc.scalar.copy, g, cut, n1)
+            nc.vector.quantize_mx(out=words[g][:, n0:n1].bitcast(FP8X4), scales=scales[4 * g:P, n0:n1], in_=grouped[g][:, n0:n1, :].rearrange("p n t -> p (n t)"))
 
         def gather_words(g, s0, s1):
             nc.vector.tensor_copy(slot_words[g][:, s0:s1], words[g][:].bitcast(U32).indirect(offs_sb[:, s0 // 16:s1 // 16]))
@@ -96,11 +101,14 @@ def tile_routed_moe_kernel(tc, xT, w_words, w_scales, b, gate, offs, pos1, pos2,
         def gather_scales(s0, s1):
             nc.vector.tensor_copy(slot_scales[:, s0:s1], scales[:].indirect(offs_sb[:, s0 // 16:s1 // 16]))
 
-        quantise(0)
+        quantise(0, 0, 256)
+        quantise(0, 1, 160)
         gather_words(0, 0, SLOTS)
-        quantise(1)
+        quantise(1, 0, 64)
+        quantise(1, 1, 64)
         gather_words(1, 0, SLOTS)
-        quantise(2)
+        quantise(2, 0, 0)
+        quantise(2, 1, 0)
         for s in range(0, SLOTS, 256):
             gather_scales(s, s + 256)
             gather_words(2, s, s + 256)
@@ -111,10 +119,11 @@ def tile_routed_moe_kernel(tc, xT, w_words, w_scales, b, gate, offs, pos1, pos2,
                 acc = psum.tile([P, C], F32, name="acc")
                 slots = slice(e * C, (e + 1) * C)
                 for a in range(PASSES):
+                    col = (3 * e + a) * N + m * P
                     nc.tensor.matmul_mx(
                         out=acc[:],
                         lhsT=w_sb[e // 2][:, 3 * (e % 2) + a, m * P:(m + 1) * P].bitcast(FP8X4),
-                        lhsT_scale=ws_u8[4 * a:P, e * N + m * P:e * N + (m + 1) * P],
+                        lhsT_scale=ws_u8[:, col:col + P],
                         rhs=slot_words[a][:, slots].bitcast(FP8X4),
                         rhs_scale=slot_scales[4 * a:P, slots],
                         start=(a == 0),
@@ -123,11 +132,11 @@ def tile_routed_moe_kernel(tc, xT, w_words, w_scales, b, gate, offs, pos1, pos2,
                 nc.scalar.activation(y[m][:, slots], acc[:], GELU, bias=b_sb[:, m, e:e + 1])
 
         for m in range(2):
-            for h0, h1 in ([(0, T)] if m == 0 else [(0, 256), (256, T)]):
+            for h0, h1 in [[(0, T)], [(0,256),(256,512)]][m]:
                 parts = []
                 for r in range(2):
                     part = keep.tile([P, h1 - h0], F32, name=f"part{m}_{h0}_{r}")
-                    nc.vector.tensor_tensor(part[:], y[m][:].indirect(pos_sb[r][:, h0 // 16:h1 // 16]), gate_sb[r][m][:, h0:h1], MULT)
+                    nc.vector.tensor_tensor(part[:], y[m][:].indirect(pos_sb[r][:, h0 // 16:h1 // 16]), gate_sb[m][:, r, h0:h1], MULT)
                     parts.append(part)
                 total = keep.tile([P, h1 - h0], F32, name=f"total{m}_{h0}")
                 nc.vector.tensor_add(total[:], parts[0][:], parts[1][:])

@@ -7,7 +7,7 @@ P = 128
 PASSES = K // 512
 SLOTS = E * C
 FLOPS = 2 * K * N * SLOTS
-WINDOW = 1376
+WINDOW = 688
 
 F32 = mybir.dt.float32
 BF16 = mybir.dt.bfloat16
@@ -42,7 +42,7 @@ def tile_routed_moe_kernel(tc, xT, w_words, w_scales, b, gate, offs, pos1, pos2,
         slot_scales = keep.tile([P, SLOTS], U8, name="slot_scales", align_bytes=64)
         w_sb = [keep.tile([P, 6, N], I32, name=f"w_sb{i}", align_bytes=64) for i in range(E // 2)]
         ws_sb = keep.tile([P, 3 * E, N // 4], I32, name="ws_sb", align_bytes=64)
-        gate_sb = [keep.tile([P, 2, T], F32, name=f"gate{m}") for m in range(2)]
+        gate_sb = [[keep.tile([P, T], F32, name=f"gate{m}_{r}") for r in range(2)] for m in range(2)]
         y = [keep.tile([P, SLOTS], F32, name=f"y{m}") for m in range(2)]
 
         nc.vector.memset(warm[:], 0.0)
@@ -53,47 +53,36 @@ def tile_routed_moe_kernel(tc, xT, w_words, w_scales, b, gate, offs, pos1, pos2,
             nc.vector.memset(words[g][:, T:], 0)
 
 
-        def load_x(g, pieces):
-            step = T // pieces
-            for n0 in range(0, T, step):
-                nc.sync.dma_start(raw[g][:, :, n0:n0 + step], x_planes[g, :, :, n0:n0 + step])
-
         def load_w(i):
             nc.sync.dma_start(w_sb[i][:], w_rows[:, 6 * i:6 * i + 6, :])
 
-        def load_ws():
-            for r in range(4):
-                nc.sync.dma_start(ws_sb[r:P:32, :, :], s_rows[r])
+        def load_gate(m, r):
+            nc.sync.dma_start(gate_sb[m][r][:], gate[r, m * P:(m + 1) * P, :])
 
-        def load_gate(m):
-            nc.sync.dma_start(gate_sb[m][:], gate[:, m * P:(m + 1) * P, :].rearrange("r p t -> p r t"))
-
-        load_x(0, 2)
+        for u in range(2):
+            nc.sync.dma_start(raw[0][:, 2 * u:2 * u + 2, :], x_planes[0, :, 2 * u:2 * u + 2, :])
         nc.sync.dma_start(offs_sb[:], offs)
-        load_x(1, 1)
-        load_x(2, 1)
+        nc.sync.dma_start(raw[1][:], x_planes[1])
+        nc.sync.dma_start(raw[2][:], x_planes[2])
         load_w(0)
-        load_ws()
-        nc.sync.dma_start(b_sb[:], b.rearrange("(m p) e -> p m e", p=P))
         load_w(1)
+        for r in range(4):
+            nc.sync.dma_start(ws_sb[r:P:32, :, :], s_rows[r])
+        nc.sync.dma_start(b_sb[:], b.rearrange("(m p) e -> p m e", p=P))
         load_w(2)
         load_w(3)
+        load_gate(0, 0)
         nc.sync.dma_start(pos_sb[0][:], pos1)
+        load_gate(0, 1)
         nc.sync.dma_start(pos_sb[1][:], pos2)
-        load_gate(0)
-        load_gate(1)
+        load_gate(1, 0)
+        load_gate(1, 1)
 
-        def interleave(copy, g, n0, n1):
-            copy(grouped[g][:, n0:n1, :].rearrange("p (c i) t -> p c t i", i=4), raw[g][:, :, n0:n1].rearrange("p t (c i) -> p c t i", i=4))
+        def interleave(copy, g, n0, n1, t0=0, t1=4):
+            copy(grouped[g][:, n0:n1, t0:t1].rearrange("p (c i) t -> p c t i", i=4), raw[g][:, t0:t1, n0:n1].rearrange("p t (c i) -> p c t i", i=4))
 
-        def quantise(g, h, on_vector):
-            n0, n1 = h * (T // 2), (h + 1) * (T // 2)
-            cut = n0 + on_vector
-            if cut > n0:
-                interleave(nc.vector.tensor_copy, g, n0, cut)
-            if cut < n1:
-                interleave(nc.scalar.copy, g, cut, n1)
-            nc.vector.quantize_mx(out=words[g][:, n0:n1].bitcast(FP8X4), scales=scales[4 * g:P, n0:n1], in_=grouped[g][:, n0:n1, :].rearrange("p n t -> p (n t)"))
+        def quantise(g):
+            nc.vector.quantize_mx(out=words[g][:, :T].bitcast(FP8X4), scales=scales[4 * g:P, :], in_=grouped[g][:].rearrange("p n t -> p (n t)"))
 
         def gather_words(g, s0, s1):
             nc.vector.tensor_copy(slot_words[g][:, s0:s1], words[g][:].bitcast(U32).indirect(offs_sb[:, s0 // 16:s1 // 16]))
@@ -101,14 +90,20 @@ def tile_routed_moe_kernel(tc, xT, w_words, w_scales, b, gate, offs, pos1, pos2,
         def gather_scales(s0, s1):
             nc.vector.tensor_copy(slot_scales[:, s0:s1], scales[:].indirect(offs_sb[:, s0 // 16:s1 // 16]))
 
-        quantise(0, 0, 256)
-        quantise(0, 1, 160)
-        gather_words(0, 0, SLOTS)
-        quantise(1, 0, 64)
-        quantise(1, 1, 64)
-        gather_words(1, 0, SLOTS)
-        quantise(2, 0, 0)
-        quantise(2, 1, 0)
+        interleave(nc.vector.tensor_copy, 0, 0, T, 0, 2)
+        interleave(nc.vector.tensor_copy, 0, 0, 352, 2, 4)
+        interleave(nc.scalar.copy, 0, 352, T, 2, 4)
+        for g, cut in ((1, 384), (2, 352)):
+            interleave(nc.scalar.copy, g, 0, cut)
+        quantise(0)
+        gather_words(0, 0, 512)
+        interleave(nc.vector.tensor_copy, 1, 384, T)
+        gather_words(0, 512, 1024)
+        quantise(1)
+        interleave(nc.vector.tensor_copy, 2, 352, T)
+        gather_words(1, 0, 512)
+        quantise(2)
+        gather_words(1, 512, 1024)
         for s in range(0, SLOTS, 256):
             gather_scales(s, s + 256)
             gather_words(2, s, s + 256)
@@ -131,13 +126,20 @@ def tile_routed_moe_kernel(tc, xT, w_words, w_scales, b, gate, offs, pos1, pos2,
                     )
                 nc.scalar.activation(y[m][:, slots], acc[:], GELU, bias=b_sb[:, m, e:e + 1])
 
-        for m in range(2):
-            for h0, h1 in [[(0, T)], [(0,256),(256,512)]][m]:
-                parts = []
-                for r in range(2):
-                    part = keep.tile([P, h1 - h0], F32, name=f"part{m}_{h0}_{r}")
-                    nc.vector.tensor_tensor(part[:], y[m][:].indirect(pos_sb[r][:, h0 // 16:h1 // 16]), gate_sb[m][:, r, h0:h1], MULT)
-                    parts.append(part)
-                total = keep.tile([P, h1 - h0], F32, name=f"total{m}_{h0}")
-                nc.vector.tensor_add(total[:], parts[0][:], parts[1][:])
-                nc.sync.dma_start(out[m * P:(m + 1) * P, h0:h1], total[:])
+        def combine(m, r, h0, h1):
+            part = keep.tile([P, h1 - h0], F32, name=f"part{m}_{r}_{h0}")
+            nc.vector.tensor_tensor(part[:], y[m][:].indirect(pos_sb[r][:, h0 // 16:h1 // 16]), gate_sb[m][r][:, h0:h1], MULT)
+            return part
+
+        def add_and_store(m, first, second, f0, h0, h1):
+            total = keep.tile([P, h1 - h0], F32, name=f"total{m}_{h0}")
+            nc.vector.tensor_add(total[:], first[:, h0 - f0:h1 - f0], second[:])
+            nc.sync.dma_start(out[m * P:(m + 1) * P, h0:h1], total[:])
+
+        first = [combine(0, 0, 0, T)]
+        second = combine(0, 1, 0, T)
+        first.append(combine(1, 0, 0, T))
+        add_and_store(0, first[0], second, 0, 0, T)
+        halves = [(h0, h1, combine(1, 1, h0, h1)) for h0, h1 in ((0, 256), (256, T))]
+        for h0, h1, half in halves:
+            add_and_store(1, first[1], half, 0, h0, h1)

from contextlib import ExitStack

import concourse.mybir as mybir

K, T, E, C, N = 1536, 512, 8, 128, 256
P = 128
PASSES = K // 512
SLOTS = E * C
FLOPS = 2 * K * N * SLOTS
WINDOW = 688

F32 = mybir.dt.float32
BF16 = mybir.dt.bfloat16
I32 = mybir.dt.int32
U32 = mybir.dt.uint32
U16 = mybir.dt.uint16
U8 = mybir.dt.uint8
FP8X4 = mybir.dt.float8_e4m3fn_x4
GELU = mybir.ActivationFunctionType.Gelu_apprx_tanh
MULT = mybir.AluOpType.mult


def tile_routed_moe_kernel(tc, xT, w_words, w_scales, b, gate, offs, pos1, pos2, out):
    nc = tc.nc
    with ExitStack() as ctx:
        keep = ctx.enter_context(tc.tile_pool(name="keep", bufs=1))
        psum = ctx.enter_context(tc.psum_pool(name="psum", bufs=8))

        x_planes = xT.rearrange("(g p t) n -> g p t n", p=P, t=4)
        w_rows = w_words.rearrange("e a p n r -> p (e a) (n r)").bitcast(I32)
        s_rows = w_scales.rearrange("e a (q r) n -> r q (e a) n", r=4).bitcast(I32)

        offs_sb = keep.tile([P, SLOTS // 16], U16, name="offs_sb")
        pos_sb = [keep.tile([P, T // 16], U16, name=f"pos{r}_sb") for r in range(2)]
        b_sb = keep.tile([P, 2, E], F32, name="b_sb")
        warm = keep.tile([P, 1], F32, name="warm")
        raw = [keep.tile([P, 4, T], F32, name=f"raw{g}") for g in range(PASSES)]
        grouped = [keep.tile([P, T, 4], BF16, name=f"grouped{g}", align_bytes=64) for g in range(PASSES)]
        words = [keep.tile([P, WINDOW], I32, name=f"words{g}", align_bytes=64) for g in range(PASSES)]
        scales = keep.tile([P, T], U8, name="scales", align_bytes=64)
        slot_words = [keep.tile([P, SLOTS], U32, name=f"slot_words{g}", align_bytes=64) for g in range(PASSES)]
        slot_scales = keep.tile([P, SLOTS], U8, name="slot_scales", align_bytes=64)
        w_sb = [keep.tile([P, 6, N], I32, name=f"w_sb{i}", align_bytes=64) for i in range(E // 2)]
        ws_sb = keep.tile([P, 3 * E, N // 4], I32, name="ws_sb", align_bytes=64)
        gate_sb = [[keep.tile([P, T], F32, name=f"gate{m}_{r}") for r in range(2)] for m in range(2)]
        y = [keep.tile([P, SLOTS], F32, name=f"y{m}") for m in range(2)]

        nc.vector.memset(warm[:], 0.0)
        nc.scalar.activation(warm[:], warm[:], GELU)
        nc.vector.memset(scales[:].bitcast(I32), 0)
        nc.vector.memset(ws_sb[:], 0)
        for g in range(PASSES):
            nc.vector.memset(words[g][:, T:], 0)


        def load_w(i):
            nc.sync.dma_start(w_sb[i][:], w_rows[:, 6 * i:6 * i + 6, :])

        def load_gate(m, r):
            nc.sync.dma_start(gate_sb[m][r][:], gate[r, m * P:(m + 1) * P, :])

        for u in range(2):
            nc.sync.dma_start(raw[0][:, 2 * u:2 * u + 2, :], x_planes[0, :, 2 * u:2 * u + 2, :])
        nc.sync.dma_start(offs_sb[:], offs)
        nc.sync.dma_start(raw[1][:], x_planes[1])
        nc.sync.dma_start(raw[2][:], x_planes[2])
        load_w(0)
        load_w(1)
        for r in range(4):
            nc.sync.dma_start(ws_sb[r:P:32, :, :], s_rows[r])
        nc.sync.dma_start(b_sb[:], b.rearrange("(m p) e -> p m e", p=P))
        load_w(2)
        load_w(3)
        load_gate(0, 0)
        nc.sync.dma_start(pos_sb[0][:], pos1)
        load_gate(0, 1)
        nc.sync.dma_start(pos_sb[1][:], pos2)
        load_gate(1, 0)
        load_gate(1, 1)

        def interleave(copy, g, n0, n1, t0=0, t1=4):
            copy(grouped[g][:, n0:n1, t0:t1].rearrange("p (c i) t -> p c t i", i=4), raw[g][:, t0:t1, n0:n1].rearrange("p t (c i) -> p c t i", i=4))

        def quantise(g):
            nc.vector.quantize_mx(out=words[g][:, :T].bitcast(FP8X4), scales=scales[4 * g:P, :], in_=grouped[g][:].rearrange("p n t -> p (n t)"))

        def gather_words(g, s0, s1):
            nc.vector.tensor_copy(slot_words[g][:, s0:s1], words[g][:].bitcast(U32).indirect(offs_sb[:, s0 // 16:s1 // 16]))

        def gather_scales(s0, s1):
            nc.vector.tensor_copy(slot_scales[:, s0:s1], scales[:].indirect(offs_sb[:, s0 // 16:s1 // 16]))

        interleave(nc.vector.tensor_copy, 0, 0, T, 0, 2)
        interleave(nc.vector.tensor_copy, 0, 0, 352, 2, 4)
        interleave(nc.scalar.copy, 0, 352, T, 2, 4)
        for g, cut in ((1, 384), (2, 352)):
            interleave(nc.scalar.copy, g, 0, cut)
        quantise(0)
        gather_words(0, 0, 512)
        interleave(nc.vector.tensor_copy, 1, 384, T)
        gather_words(0, 512, 1024)
        quantise(1)
        interleave(nc.vector.tensor_copy, 2, 352, T)
        gather_words(1, 0, 512)
        quantise(2)
        gather_words(1, 512, 1024)
        for s in range(0, SLOTS, 256):
            gather_scales(s, s + 256)
            gather_words(2, s, s + 256)

        ws_u8 = ws_sb[:].rearrange("p e n -> p (e n)").bitcast(U8)
        for m in range(2):
            for e in range(E):
                acc = psum.tile([P, C], F32, name="acc")
                slots = slice(e * C, (e + 1) * C)
                for a in range(PASSES):
                    col = (3 * e + a) * N + m * P
                    nc.tensor.matmul_mx(
                        out=acc[:],
                        lhsT=w_sb[e // 2][:, 3 * (e % 2) + a, m * P:(m + 1) * P].bitcast(FP8X4),
                        lhsT_scale=ws_u8[:, col:col + P],
                        rhs=slot_words[a][:, slots].bitcast(FP8X4),
                        rhs_scale=slot_scales[4 * a:P, slots],
                        start=(a == 0),
                        stop=(a == PASSES - 1),
                    )
                nc.scalar.activation(y[m][:, slots], acc[:], GELU, bias=b_sb[:, m, e:e + 1])

        def combine(m, r, h0, h1):
            part = keep.tile([P, h1 - h0], F32, name=f"part{m}_{r}_{h0}")
            nc.vector.tensor_tensor(part[:], y[m][:].indirect(pos_sb[r][:, h0 // 16:h1 // 16]), gate_sb[m][r][:, h0:h1], MULT)
            return part

        def add_and_store(m, first, second, f0, h0, h1):
            total = keep.tile([P, h1 - h0], F32, name=f"total{m}_{h0}")
            nc.vector.tensor_add(total[:], first[:, h0 - f0:h1 - f0], second[:])
            nc.sync.dma_start(out[m * P:(m + 1) * P, h0:h1], total[:])

        first = [combine(0, 0, 0, T)]
        second = combine(0, 1, 0, T)
        first.append(combine(1, 0, 0, T))
        add_and_store(0, first[0], second, 0, 0, T)
        halves = [(h0, h1, combine(1, 1, h0, h1)) for h0, h1 in ((0, 256), (256, T))]
        for h0, h1, half in halves:
            add_and_store(1, first[1], half, 0, h0, h1)
